import numpy as np
import ml_dtypes


def mxq(x, axis, fmt="e4m3"):
    dtype, down = {"e4m3": (ml_dtypes.float8_e4m3fn, 7), "e5m2": (ml_dtypes.float8_e5m2, 14)}[fmt]
    v = np.moveaxis(np.asarray(x, np.float32).astype(ml_dtypes.bfloat16).astype(np.float64), axis, -1)
    blocks = v.reshape(v.shape[:-1] + (-1, 32))
    amax = np.abs(blocks).max(-1, keepdims=True)
    byte = np.maximum(np.where(amax > 0, np.frexp(amax)[1] - 1 + 127, 0) - down, 1)
    scale = np.exp2(byte - 127.0)
    codes = (blocks / scale).astype(np.float32).astype(dtype).astype(np.float64)
    return np.moveaxis((codes * scale).reshape(v.shape), -1, axis)


WIDE = False


def mx_kscale(k):
    if not WIDE:
        return np.ones(k)
    levels = np.array([10, -10, 5, -5, 0])
    if k % 512:
        return np.exp2(np.random.permutation(np.resize(levels, k // 32))).repeat(32)
    a = np.empty((k // 512, 16))
    for p in range(k // 512):
        a[p, :8] = np.random.permutation(np.resize(levels, 8))
        for g in range(8):
            far = levels[np.abs(levels - a[p, g]) >= 10]
            a[p, g + 8] = far[np.random.randint(len(far))]
    return np.exp2(a.ravel()).repeat(32)


def f64(x):
    return np.asarray(x).astype(np.float64)


def striped(idx):
    return np.tile(idx.reshape(-1, 16).T, (8, 1)).astype(np.uint16)


def unstriped(offs):
    return offs[:16].T.reshape(-1).astype(np.int64)


def pack_weight(w):
    k, n = w.shape
    w = f64(np.asarray(w, np.float32).astype(ml_dtypes.bfloat16)).reshape(k // 32, 32, n)
    amax = np.abs(w).max(1)
    byte = np.clip(np.where(amax > 0, np.frexp(amax)[1] - 1 + 127 - 7, 1), 1, 254)
    scaled = (w * np.exp2(127.0 - byte)[:, None, :]).reshape(k, n).astype(np.float32)
    words = np.ascontiguousarray(scaled.reshape(k // 512, 128, 4, n).transpose(0, 1, 3, 2)).astype(ml_dtypes.float8_e4m3fn).view(np.uint8)
    return words, np.ascontiguousarray(byte.astype(np.uint8).reshape(k // 512, 16, n))


def unpack_weight(words, scales):
    g, p, n, _ = words.shape
    vals = np.ascontiguousarray(words).view(ml_dtypes.float8_e4m3fn).astype(np.float64) * np.repeat(np.exp2(scales.astype(np.float64) - 127.0), 8, axis=1)[..., None]
    return vals.transpose(0, 1, 3, 2).reshape(g * 512, n)


def sigmoid(v):
    return 1.0 / (1.0 + np.exp(-np.maximum(v, -700.0)))

def planes(y):
    n, m = y.shape
    v = y.astype(np.float32).astype(ml_dtypes.bfloat16).astype(np.float64).reshape(n // 32, 32, m)
    top = np.abs(v).max(1)
    byte = np.clip(np.where(top > 0, np.frexp(top)[1] - 1 + 127 - 7, 1), 1, 254)
    codes = (v * np.exp2(127.0 - byte)[:, None, :]).reshape(n, m).astype(np.float32).astype(ml_dtypes.float8_e4m3fn).view(np.uint8)
    words = codes.reshape(n // 512, 128, 4, m).transpose(0, 1, 3, 2)
    return np.ascontiguousarray(words), np.ascontiguousarray(byte.astype(np.uint8).reshape(n // 512, 16, m))


K, T, N, U = 512, 512, 512, 1024


def setup_inputs():
    n = np.random.standard_normal
    s = mx_kscale(K)[:, None]
    packed_xT = pack_weight(n((K, T)) * s)
    return {
        "x_words": packed_xT[0],
        "x_scales": packed_xT[1],
        "mem": n((N, U)).astype(np.float32),
        "w1": (n((K, N)) / np.sqrt(K) / s).astype(np.float32),
        "w2": (n((K, N)) / np.sqrt(K) / s).astype(np.float32),
        "slot": striped(np.random.permutation(U)[:T]),
    }


def reference(x_words, x_scales, mem, w1, w2, slot):
    old = f64(mem)[:, unstriped(slot)]
    xq = unpack_weight(x_words, x_scales)
    g = sigmoid(mxq(f64(w2), 0, "e4m3").T @ xq)
    y = np.tanh(mxq(f64(w1), 0, "e4m3").T @ xq)
    out = f64(mem).copy()
    out[:, unstriped(slot)] = old + g * (y - old)
    return (out,) + planes(out)

@@ -1,0 +1,172 @@
+from contextlib import ExitStack
+
+import concourse.mybir as mybir
+
+K, T, N, U = 512, 512, 512, 1024
+FLOPS = 2 * 2 * K * N * T
+
+F32 = mybir.dt.float32
+BF16 = mybir.dt.bfloat16
+I32 = mybir.dt.int32
+U32 = mybir.dt.uint32
+U16 = mybir.dt.uint16
+U8 = mybir.dt.uint8
+FP8X4 = mybir.dt.float8_e4m3fn_x4
+ALU = mybir.AluOpType
+ACT = mybir.ActivationFunctionType
+
+P = 128
+PACK = 4
+QUADRANTS = 4
+QUADRANT = 32
+SCALE_ROWS = 4
+PAIR = 2
+OUT_CHUNKS = ((0, 512), (512, 768), (768, 1024))
+
+
+def tile_picked_wgmem_tanh_lo_kernel(
+    tc, x_words, x_scales, mem, w1, w2, slot, out_0, out_1, out_2
+):
+    nc = tc.nc
+    mem_rows = mem.rearrange("(p t) u -> p t u", t=PACK)
+    out_rows = out_0.rearrange("(p t) u -> p t u", t=PACK)
+    out_words = out_1[0].rearrange("p u r -> p (u r)").bitcast(I32)
+
+    with ExitStack() as ctx:
+        keep = ctx.enter_context(tc.tile_pool(name="keep", bufs=1))
+        psum = ctx.enter_context(tc.psum_pool(name="psum", bufs=1))
+
+        offsets = keep.tile([P, T // 16], U16, name="offsets")
+        window = [keep.tile([P, U], F32, name="window%d" % t) for t in range(PACK)]
+        raw = {"gate": keep.tile([P, PACK, N], F32, name="raw_gate"), "cand": keep.tile([P, PACK, N], F32, name="raw_cand")}
+        x_codes = keep.tile([P, T], U32, name="x_codes", align_bytes=64)
+        x_plane = keep.tile([P, T], U8, name="x_plane", align_bytes=64)
+
+        def load_weight(which, w):
+            nc.sync.dma_start(raw[which][:], w.rearrange("(p j) m -> p j m", j=PACK))
+
+        def load_window(t):
+            nc.sync.dma_start(window[t][:], mem_rows[:, t, :])
+
+        nc.gpsimd.memset(x_plane[:].bitcast(U32), 0)
+        for q in range(QUADRANTS):
+            nc.scalar.dma_start(
+                x_plane[QUADRANT * q : QUADRANT * q + SCALE_ROWS, :].bitcast(I32),
+                x_scales[0, SCALE_ROWS * q : SCALE_ROWS * (q + 1), :].bitcast(I32),
+            )
+
+        load_window(0)
+        nc.sync.dma_start(offsets[:], slot)
+        load_weight("gate", w2)
+        nc.sync.dma_start(x_codes[:].bitcast(I32), x_words[0].rearrange("p n r -> p (n r)").bitcast(I32))
+        load_window(1)
+        load_weight("cand", w1)
+        load_window(2)
+        load_window(3)
+
+        dealt, codes, plane, acc = {}, {}, {}, {}
+
+        def deal(which, half, copy):
+            dealt[which, half] = keep.tile([P, PAIR, P, PACK], BF16, name="dealt_%s%d" % (which, half), align_bytes=64)
+            copy(
+                dealt[which, half][:].rearrange("p t m j -> p m j t"),
+                raw[which][:].rearrange("p j (m t) -> p m j t", t=PACK)[:, :, :, PAIR * half : PAIR * (half + 1)],
+            )
+
+        def quantize_weight(which, half):
+            codes[which, half] = keep.tile([P, PAIR * P], U32, name="codes_%s%d" % (which, half), align_bytes=64)
+            plane[which, half] = keep.tile([P, PAIR * P], U8, name="plane_%s%d" % (which, half), align_bytes=64)
+            nc.vector.quantize_mx(
+                out=codes[which, half][:].bitcast(FP8X4),
+                scales=plane[which, half][:],
+                in_=dealt[which, half][:].rearrange("p t m j -> p (t m j)"),
+            )
+
+        def multiply(which, t):
+            half, cols = t // PAIR, slice(P * (t % PAIR), P * (t % PAIR + 1))
+            acc[which, t] = psum.tile([P, T], F32, name="acc_%s%d" % (which, t))
+            nc.tensor.matmul_mx(
+                out=acc[which, t][:],
+                lhsT=codes[which, half][:, cols].bitcast(FP8X4),
+                lhsT_scale=plane[which, half][:, cols],
+                rhs=x_codes[:].bitcast(FP8X4),
+                rhs_scale=x_plane[:],
+                start=True,
+                stop=True,
+            )
+
+        stay = [keep.tile([P, T], F32, name="stay%d" % t) for t in range(PACK)]
+        cand = [keep.tile([P, T], F32, name="cand%d" % t) for t in range(PACK)]
+        old = [keep.tile([P, T], F32, name="old%d" % t) for t in range(PACK)]
+        kept = [keep.tile([P, T], F32, name="kept%d" % t) for t in range(PACK)]
+        moved = [keep.tile([P, T], F32, name="moved%d" % t) for t in range(PACK)]
+        new = [keep.tile([P, T], F32, name="new%d" % t) for t in range(PACK)]
+        rounded = [
+            keep.tile([P, hi - lo, PACK], BF16, name="rounded%d" % c, align_bytes=64) for c, (lo, hi) in enumerate(OUT_CHUNKS)
+        ]
+        words = [keep.tile([P, hi - lo], U32, name="words%d" % c, align_bytes=64) for c, (lo, hi) in enumerate(OUT_CHUNKS)]
+        out_plane = keep.tile([P, U], U8, name="out_plane", align_bytes=64)
+
+        def gather(t):
+            nc.vector.tensor_copy(old[t][:], window[t][:].indirect(offsets[:]))
+
+        def keep_share(t):
+            nc.vector.tensor_tensor(kept[t][:], old[t][:], stay[t][:], ALU.mult)
+
+        def write_back(t):
+            nc.vector.scalar_tensor_tensor(moved[t][:], stay[t][:], 1.0, cand[t][:], ALU.subtract, ALU.mult)
+            nc.vector.tensor_tensor(new[t][:], kept[t][:], moved[t][:], ALU.subtract)
+            nc.vector.tensor_copy(window[t][:].indirect(offsets[:]), new[t][:])
+            nc.sync.dma_start(out_rows[:, t, :], window[t][:])
+
+        def round_out(t, c, copy):
+            lo, hi = OUT_CHUNKS[c]
+            if (t, c) == (PACK - 2, 0):
+                both = window[t][:, lo:hi].rearrange("p (u o) -> p u o", o=1).to_broadcast([P, hi - lo, PAIR])
+                copy(rounded[c][:, :, t:], both)
+            else:
+                copy(rounded[c][:, :, t], window[t][:, lo:hi])
+
+        gather(0)
+        deal("gate", 0, nc.vector.tensor_copy)
+        deal("gate", 1, nc.scalar.copy)
+        for half in range(2):
+            quantize_weight("gate", half)
+        for t in range(PACK):
+            multiply("gate", t)
+            nc.scalar.activation(stay[t][:], acc["gate", t][:], ACT.Sigmoid, scale=-1.0)
+        gather(1)
+        keep_share(0)
+        keep_share(1)
+        deal("cand", 0, nc.vector.tensor_copy)
+        deal("cand", 1, nc.scalar.copy)
+        for half in range(2):
+            quantize_weight("cand", half)
+        for t in range(PACK):
+            multiply("cand", t)
+            nc.scalar.activation(cand[t][:], acc["cand", t][:], ACT.Tanh)
+        for t in range(PACK):
+            if t >= 2:
+                gather(t)
+                keep_share(t)
+            write_back(t)
+            if t < PACK - 1:
+                for c in range(len(OUT_CHUNKS)):
+                    round_out(t, c, nc.scalar.copy)
+
+        round_out(PACK - 1, 0, nc.vector.tensor_copy)
+        for c in range(1, len(OUT_CHUNKS)):
+            round_out(PACK - 1, c, nc.scalar.copy)
+        for c, (lo, hi) in enumerate(OUT_CHUNKS):
+            nc.vector.quantize_mx(
+                out=words[c][:].bitcast(FP8X4),
+                scales=out_plane[:, lo:hi],
+                in_=rounded[c][:].rearrange("p u t -> p (u t)"),
+            )
+            nc.sync.dma_start(out_words[:, lo:hi], words[c][:].bitcast(I32))
+        for q in range(QUADRANTS):
+            queue = nc.sync if q % 2 == 0 else nc.scalar
+            queue.dma_start(
+                out_2[0, SCALE_ROWS * q : SCALE_ROWS * (q + 1), :].bitcast(I32),
+                out_plane[QUADRANT * q : QUADRANT * q + SCALE_ROWS, :].bitcast(I32),
+            )

@@ -21,7 +21,7 @@ QUADRANTS = 4
 QUADRANT = 32
 SCALE_ROWS = 4
 PAIR = 2
-OUT_CHUNKS = ((0, 512), (512, 768), (768, 1024))
+OUT_CHUNKS = ((0, 512), (512, 1024))
 
 
 def tile_picked_wgmem_tanh_lo_kernel(
@@ -38,69 +38,83 @@ def tile_picked_wgmem_tanh_lo_kernel(
 
         offsets = keep.tile([P, T // 16], U16, name="offsets")
         window = [keep.tile([P, U], F32, name="window%d" % t) for t in range(PACK)]
-        raw = {"gate": keep.tile([P, PACK, N], F32, name="raw_gate"), "cand": keep.tile([P, PACK, N], F32, name="raw_cand")}
+        pieces = {"gate": 1, "cand": 2}
+        raw = {
+            (which, i): keep.tile([P, PACK, N // n], F32, name="raw_%s%d" % (which, i))
+            for which, n in (("gate", 1), ("cand", 2))
+            for i in range(n)
+        }
         x_codes = keep.tile([P, T], U32, name="x_codes", align_bytes=64)
         x_plane = keep.tile([P, T], U8, name="x_plane", align_bytes=64)
 
         def load_weight(which, w):
-            nc.sync.dma_start(raw[which][:], w.rearrange("(p j) m -> p j m", j=PACK))
+            width = N // pieces[which]
+            for i in range(pieces[which]):
+                nc.sync.dma_start(
+                    raw[which, i][:], w.rearrange("(p j) m -> p j m", j=PACK)[:, :, width * i : width * (i + 1)]
+                )
 
         def load_window(t):
             nc.sync.dma_start(window[t][:], mem_rows[:, t, :])
 
-        nc.gpsimd.memset(x_plane[:].bitcast(U32), 0)
+        nc.vector.memset(x_plane[:].bitcast(U32), 0)
+        nc.sync.dma_start(offsets[:], slot)
+        load_weight("gate", w2)
         for q in range(QUADRANTS):
-            nc.scalar.dma_start(
+            nc.sync.dma_start(
                 x_plane[QUADRANT * q : QUADRANT * q + SCALE_ROWS, :].bitcast(I32),
                 x_scales[0, SCALE_ROWS * q : SCALE_ROWS * (q + 1), :].bitcast(I32),
             )
-
-        load_window(0)
-        nc.sync.dma_start(offsets[:], slot)
-        load_weight("gate", w2)
         nc.sync.dma_start(x_codes[:].bitcast(I32), x_words[0].rearrange("p n r -> p (n r)").bitcast(I32))
-        load_window(1)
+        for t in range(PACK - 1):
+            load_window(t)
         load_weight("cand", w1)
-        load_window(2)
-        load_window(3)
+        load_window(PACK - 1)
 
+        span = {"gate": PACK, "cand": PAIR}
         dealt, codes, plane, acc = {}, {}, {}, {}
+        for which in ("gate", "cand"):
+            for g in range(PACK // span[which]):
+                label = "%s%d" % (which, g)
+                dealt[which, g] = keep.tile([P, span[which], P, PACK], BF16, name="dealt_" + label, tag="dealt_" + label, align_bytes=64)
+                codes[which, g] = keep.tile([P, span[which] * P], U32, name="codes_" + label, align_bytes=64)
+                if label != "cand1":
+                    plane[which, g] = keep.tile([P, span[which] * P], U8, name="plane_" + label, align_bytes=64)
 
-        def deal(which, half, copy):
-            dealt[which, half] = keep.tile([P, PAIR, P, PACK], BF16, name="dealt_%s%d" % (which, half), align_bytes=64)
+        def deal(which, g, piece, lo, hi, copy):
+            first = piece * (P // pieces[which])
             copy(
-                dealt[which, half][:].rearrange("p t m j -> p m j t"),
-                raw[which][:].rearrange("p j (m t) -> p m j t", t=PACK)[:, :, :, PAIR * half : PAIR * (half + 1)],
+                dealt[which, g][:].rearrange("p t m j -> p m j t")[:, first + lo : first + hi],
+                raw[which, piece][:].rearrange("p j (m t) -> p m j t", t=PACK)[:, lo:hi, :, span[which] * g : span[which] * (g + 1)],
             )
 
-        def quantize_weight(which, half):
-            codes[which, half] = keep.tile([P, PAIR * P], U32, name="codes_%s%d" % (which, half), align_bytes=64)
-            plane[which, half] = keep.tile([P, PAIR * P], U8, name="plane_%s%d" % (which, half), align_bytes=64)
+        def quantize_weight(which, g):
             nc.vector.quantize_mx(
-                out=codes[which, half][:].bitcast(FP8X4),
-                scales=plane[which, half][:],
-                in_=dealt[which, half][:].rearrange("p t m j -> p (t m j)"),
+                out=codes[which, g][:].bitcast(FP8X4),
+                scales=plane[which, g][:],
+                in_=dealt[which, g][:].rearrange("p t m j -> p (t m j)"),
             )
 
         def multiply(which, t):
-            half, cols = t // PAIR, slice(P * (t % PAIR), P * (t % PAIR + 1))
+            g, cols = t // span[which], slice(P * (t % span[which]), P * (t % span[which] + 1))
             acc[which, t] = psum.tile([P, T], F32, name="acc_%s%d" % (which, t))
             nc.tensor.matmul_mx(
                 out=acc[which, t][:],
-                lhsT=codes[which, half][:, cols].bitcast(FP8X4),
-                lhsT_scale=plane[which, half][:, cols],
+                lhsT=codes[which, g][:, cols].bitcast(FP8X4),
+                lhsT_scale=plane[which, g][:, cols],
                 rhs=x_codes[:].bitcast(FP8X4),
                 rhs_scale=x_plane[:],
                 start=True,
                 stop=True,
             )
 
-        stay = [keep.tile([P, T], F32, name="stay%d" % t) for t in range(PACK)]
+        stay = [keep.tile([P, T], F32, name="stay%d" % t, tag="stay%d" % t, align_bytes=64) for t in range(PACK)]
         cand = [keep.tile([P, T], F32, name="cand%d" % t) for t in range(PACK)]
-        old = [keep.tile([P, T], F32, name="old%d" % t) for t in range(PACK)]
-        kept = [keep.tile([P, T], F32, name="kept%d" % t) for t in range(PACK)]
-        moved = [keep.tile([P, T], F32, name="moved%d" % t) for t in range(PACK)]
         new = [keep.tile([P, T], F32, name="new%d" % t) for t in range(PACK)]
+        old = [keep.tile([P, T], F32, name="old%d" % t) for t in range(PACK)]
+        kept = {t: keep.tile([P, T], F32, name="kept%d" % t, tag="kept%d" % t) for t in (0, 1, 3)}
+        gate = {}
+        moved = keep.tile([P, T], F32, name="moved")
         rounded = [
             keep.tile([P, hi - lo, PACK], BF16, name="rounded%d" % c, align_bytes=64) for c, (lo, hi) in enumerate(OUT_CHUNKS)
         ]
@@ -110,12 +124,7 @@ def tile_picked_wgmem_tanh_lo_kernel(
         def gather(t):
             nc.vector.tensor_copy(old[t][:], window[t][:].indirect(offsets[:]))
 
-        def keep_share(t):
-            nc.vector.tensor_tensor(kept[t][:], old[t][:], stay[t][:], ALU.mult)
-
         def write_back(t):
-            nc.vector.scalar_tensor_tensor(moved[t][:], stay[t][:], 1.0, cand[t][:], ALU.subtract, ALU.mult)
-            nc.vector.tensor_tensor(new[t][:], kept[t][:], moved[t][:], ALU.subtract)
             nc.vector.tensor_copy(window[t][:].indirect(offsets[:]), new[t][:])
             nc.sync.dma_start(out_rows[:, t, :], window[t][:])
 
@@ -127,43 +136,70 @@ def tile_picked_wgmem_tanh_lo_kernel(
             else:
                 copy(rounded[c][:, :, t], window[t][:, lo:hi])
 
-        gather(0)
-        deal("gate", 0, nc.vector.tensor_copy)
-        deal("gate", 1, nc.scalar.copy)
-        for half in range(2):
-            quantize_weight("gate", half)
+        last = PACK - 1
+        deal("gate", 0, 0, 0, 96, nc.vector.tensor_copy)
+        deal("gate", 0, 0, 96, P, nc.scalar.copy)
+        quantize_weight("gate", 0)
         for t in range(PACK):
             multiply("gate", t)
             nc.scalar.activation(stay[t][:], acc["gate", t][:], ACT.Sigmoid, scale=-1.0)
-        gather(1)
-        keep_share(0)
-        keep_share(1)
-        deal("cand", 0, nc.vector.tensor_copy)
-        deal("cand", 1, nc.scalar.copy)
-        for half in range(2):
-            quantize_weight("cand", half)
-        for t in range(PACK):
+        gate[1] = keep.tile([P, T], F32, name="gate1")
+        nc.scalar.activation(gate[1][:], acc["gate", 1][:], ACT.Sigmoid)
+        for t in range(last):
+            gather(t)
+        for t in range(2):
+            nc.gpsimd.tensor_tensor(kept[t][:], old[t][:], stay[t][:], ALU.mult)
+        for piece in range(2):
+            deal("cand", 0, piece, 0, P // 2, nc.vector.tensor_copy)
+            deal("cand", 1, piece, 0, P // 2, nc.scalar.copy)
+        quantize_weight("cand", 0)
+        kept[2] = keep.tile([P, T], F32, name="kept2", tag="dealt_cand0", align_bytes=64)
+        nc.gpsimd.tensor_tensor(kept[2][:], old[2][:], stay[2][:], ALU.mult)
+        gather(last)
+        plane["cand", 1] = keep.tile([P, PAIR * P], U8, name="plane_cand1", tag="stay2", align_bytes=64)
+        quantize_weight("cand", 1)
+
+        def candidate(t):
             multiply("cand", t)
             nc.scalar.activation(cand[t][:], acc["cand", t][:], ACT.Tanh)
+
+        for t in range(PAIR):
+            candidate(t)
+        nc.vector.scalar_tensor_tensor(moved[:], stay[0][:], 1.0, cand[0][:], ALU.subtract, ALU.mult)
+        for t in range(PAIR, PACK):
+            candidate(t)
         for t in range(PACK):
-            if t >= 2:
-                gather(t)
-                keep_share(t)
+            if t == 0:
+                nc.vector.tensor_tensor(new[t][:], kept[t][:], moved[:], ALU.subtract)
+                gate[2] = keep.tile([P, T], F32, name="gate2", tag="kept0")
+                nc.scalar.activation(gate[2][:], acc["gate", 2][:], ACT.Sigmoid)
+            elif t < last:
+                nc.gpsimd.tensor_tensor(moved[:], gate[t][:], cand[t][:], ALU.mult)
+                nc.gpsimd.tensor_tensor(new[t][:], kept[t][:], moved[:], ALU.add)
+            else:
+                nc.gpsimd.tensor_tensor(moved[:], old[t][:], cand[t][:], ALU.subtract)
+                nc.gpsimd.tensor_tensor(kept[t][:], moved[:], stay[t][:], ALU.mult)
+                nc.gpsimd.tensor_tensor(new[t][:], kept[t][:], cand[t][:], ALU.add)
             write_back(t)
-            if t < PACK - 1:
+            if t < last:
                 for c in range(len(OUT_CHUNKS)):
                     round_out(t, c, nc.scalar.copy)
 
-        round_out(PACK - 1, 0, nc.vector.tensor_copy)
-        for c in range(1, len(OUT_CHUNKS)):
-            round_out(PACK - 1, c, nc.scalar.copy)
+        for c, copy in enumerate((nc.vector.tensor_copy, nc.scalar.copy)):
+            lo, hi = OUT_CHUNKS[c]
+            for first in range(0, hi - lo, 256):
+                copy(rounded[c][:, first : first + 256, last], window[last][:, lo + first : lo + first + 256])
         for c, (lo, hi) in enumerate(OUT_CHUNKS):
-            nc.vector.quantize_mx(
-                out=words[c][:].bitcast(FP8X4),
-                scales=out_plane[:, lo:hi],
-                in_=rounded[c][:].rearrange("p u t -> p (u t)"),
-            )
-            nc.sync.dma_start(out_words[:, lo:hi], words[c][:].bitcast(I32))
+            for first in range(0, hi - lo, 256):
+                nc.vector.quantize_mx(
+                    out=words[c][:, first : first + 256].bitcast(FP8X4),
+                    scales=out_plane[:, lo + first : lo + first + 256],
+                    in_=rounded[c][:, first : first + 256, :].rearrange("p u t -> p (u t)"),
+                )
+                if c == 1:
+                    nc.sync.dma_start(out_words[:, lo + first : lo + first + 256], words[c][:, first : first + 256].bitcast(I32))
+            if c == 0:
+                nc.sync.dma_start(out_words[:, lo:hi], words[c][:].bitcast(I32))
         for q in range(QUADRANTS):
             queue = nc.sync if q % 2 == 0 else nc.scalar
             queue.dma_start(

@@ -38,37 +38,36 @@ def tile_picked_wgmem_tanh_lo_kernel(
 
         offsets = keep.tile([P, T // 16], U16, name="offsets")
         window = [keep.tile([P, U], F32, name="window%d" % t) for t in range(PACK)]
-        pieces = {"gate": 1, "cand": 2}
         raw = {
-            (which, i): keep.tile([P, PACK, N // n], F32, name="raw_%s%d" % (which, i))
-            for which, n in (("gate", 1), ("cand", 2))
-            for i in range(n)
+            (which, piece): keep.tile([P, PAIR, N], F32, name="raw_%s%d" % (which, piece))
+            for which in ("gate", "cand")
+            for piece in range(2)
         }
         x_codes = keep.tile([P, T], U32, name="x_codes", align_bytes=64)
         x_plane = keep.tile([P, T], U8, name="x_plane", align_bytes=64)
 
-        def load_weight(which, w):
-            width = N // pieces[which]
-            for i in range(pieces[which]):
-                nc.sync.dma_start(
-                    raw[which, i][:], w.rearrange("(p j) m -> p j m", j=PACK)[:, :, width * i : width * (i + 1)]
-                )
+        def load_weight(which, w, piece):
+            nc.sync.dma_start(
+                raw[which, piece][:], w.rearrange("(p j) m -> p j m", j=PACK)[:, PAIR * piece : PAIR * (piece + 1), :]
+            )
 
         def load_window(t):
             nc.sync.dma_start(window[t][:], mem_rows[:, t, :])
 
         nc.vector.memset(x_plane[:].bitcast(U32), 0)
         nc.sync.dma_start(offsets[:], slot)
-        load_weight("gate", w2)
+        load_weight("gate", w2, 0)
         for q in range(QUADRANTS):
             nc.sync.dma_start(
                 x_plane[QUADRANT * q : QUADRANT * q + SCALE_ROWS, :].bitcast(I32),
                 x_scales[0, SCALE_ROWS * q : SCALE_ROWS * (q + 1), :].bitcast(I32),
             )
+        load_weight("gate", w2, 1)
         nc.sync.dma_start(x_codes[:].bitcast(I32), x_words[0].rearrange("p n r -> p (n r)").bitcast(I32))
         for t in range(PACK - 1):
             load_window(t)
-        load_weight("cand", w1)
+        for piece in range(2):
+            load_weight("cand", w1, piece)
         load_window(PACK - 1)
 
         span = {"gate": PACK, "cand": PAIR}
@@ -82,9 +81,8 @@ def tile_picked_wgmem_tanh_lo_kernel(
                     plane[which, g] = keep.tile([P, span[which] * P], U8, name="plane_" + label, align_bytes=64)
 
         def deal(which, g, piece, lo, hi, copy):
-            first = piece * (P // pieces[which])
             copy(
-                dealt[which, g][:].rearrange("p t m j -> p m j t")[:, first + lo : first + hi],
+                dealt[which, g][:].rearrange("p t m j -> p m j t")[:, lo:hi, PAIR * piece : PAIR * (piece + 1), :],
                 raw[which, piece][:].rearrange("p j (m t) -> p m j t", t=PACK)[:, lo:hi, :, span[which] * g : span[which] * (g + 1)],
             )
 
@@ -108,11 +106,12 @@ def tile_picked_wgmem_tanh_lo_kernel(
                 stop=True,
             )
 
-        stay = [keep.tile([P, T], F32, name="stay%d" % t, tag="stay%d" % t, align_bytes=64) for t in range(PACK)]
-        cand = [keep.tile([P, T], F32, name="cand%d" % t) for t in range(PACK)]
+        left = keep.tile([P, PAIR, T], F32, name="left")
+        stay = [keep.tile([P, T], F32, name="stay%d" % t, tag="stay%d" % t, align_bytes=64) for t in range(PACK - 1)]
+        cand = [keep.tile([P, T], F32, name="cand%d" % t) for t in range(PACK - 1)] + [left[:, 1, :]]
         new = [keep.tile([P, T], F32, name="new%d" % t) for t in range(PACK)]
-        old = [keep.tile([P, T], F32, name="old%d" % t) for t in range(PACK)]
-        kept = {t: keep.tile([P, T], F32, name="kept%d" % t, tag="kept%d" % t) for t in (0, 1, 3)}
+        old = [keep.tile([P, T], F32, name="old%d" % t) for t in range(PACK - 1)] + [left[:, 0, :]]
+        kept = {t: keep.tile([P, T], F32, name="kept%d" % t, tag="kept%d" % t) for t in (0, 1)}
         gate = {}
         moved = keep.tile([P, T], F32, name="moved")
         rounded = [
@@ -137,21 +136,23 @@ def tile_picked_wgmem_tanh_lo_kernel(
                 copy(rounded[c][:, :, t], window[t][:, lo:hi])
 
         last = PACK - 1
-        deal("gate", 0, 0, 0, 96, nc.vector.tensor_copy)
-        deal("gate", 0, 0, 96, P, nc.scalar.copy)
+        for piece in range(2):
+            deal("gate", 0, piece, 0, 96, nc.vector.tensor_copy)
+            deal("gate", 0, piece, 96, P, nc.scalar.copy)
         quantize_weight("gate", 0)
         for t in range(PACK):
             multiply("gate", t)
-            nc.scalar.activation(stay[t][:], acc["gate", t][:], ACT.Sigmoid, scale=-1.0)
+            if t < last:
+                nc.scalar.activation(stay[t][:], acc["gate", t][:], ACT.Sigmoid, scale=-1.0)
         gate[1] = keep.tile([P, T], F32, name="gate1")
         nc.scalar.activation(gate[1][:], acc["gate", 1][:], ACT.Sigmoid)
         for t in range(last):
             gather(t)
         for t in range(2):
             nc.gpsimd.tensor_tensor(kept[t][:], old[t][:], stay[t][:], ALU.mult)
-        for piece in range(2):
-            deal("cand", 0, piece, 0, P // 2, nc.vector.tensor_copy)
-            deal("cand", 1, piece, 0, P // 2, nc.scalar.copy)
+        for piece, copy in enumerate((nc.scalar.copy, nc.vector.tensor_copy)):
+            for g in range(2):
+                deal("cand", g, piece, 0, P, copy)
         quantize_weight("cand", 0)
         kept[2] = keep.tile([P, T], F32, name="kept2", tag="dealt_cand0", align_bytes=64)
         nc.gpsimd.tensor_tensor(kept[2][:], old[2][:], stay[2][:], ALU.mult)
@@ -173,13 +174,16 @@ def tile_picked_wgmem_tanh_lo_kernel(
                 nc.vector.tensor_tensor(new[t][:], kept[t][:], moved[:], ALU.subtract)
                 gate[2] = keep.tile([P, T], F32, name="gate2", tag="kept0")
                 nc.scalar.activation(gate[2][:], acc["gate", 2][:], ACT.Sigmoid)
+                right = keep.tile([P, PAIR, T], F32, name="right", tag="stay0", align_bytes=64)
+                nc.scalar.activation(right[:, 0, :], acc["gate", last][:], ACT.Sigmoid, scale=-1.0)
+                nc.scalar.activation(right[:, 1, :], acc["gate", last][:], ACT.Sigmoid)
             elif t < last:
                 nc.gpsimd.tensor_tensor(moved[:], gate[t][:], cand[t][:], ALU.mult)
                 nc.gpsimd.tensor_tensor(new[t][:], kept[t][:], moved[:], ALU.add)
             else:
-                nc.gpsimd.tensor_tensor(moved[:], old[t][:], cand[t][:], ALU.subtract)
-                nc.gpsimd.tensor_tensor(kept[t][:], moved[:], stay[t][:], ALU.mult)
-                nc.gpsimd.tensor_tensor(new[t][:], kept[t][:], cand[t][:], ALU.add)
+                shares = keep.tile([P, PAIR, T], F32, name="shares", tag="dealt_cand0", align_bytes=64)
+                nc.gpsimd.tensor_tensor(shares[:], left[:], right[:], ALU.mult)
+                nc.gpsimd.tensor_tensor(new[t][:], shares[:, 0, :], shares[:, 1, :], ALU.add)
             write_back(t)
             if t < last:
                 for c in range(len(OUT_CHUNKS)):

@@ -187,7 +187,12 @@ def tile_picked_wgmem_tanh_lo_kernel(
             write_back(t)
             if t < last:
                 for c in range(len(OUT_CHUNKS)):
-                    round_out(t, c, nc.scalar.copy)
+                    if (t, c) != (last - 1, 1):
+                        round_out(t, c, nc.scalar.copy)
+        one = keep.tile([P, 1], F32, name="one", tag="dealt_cand0", align_bytes=64)
+        nc.gpsimd.memset(one[:], 1.0)
+        both = window[last - 1][:, 512:].rearrange("p (u o) -> p u o", o=1).to_broadcast([P, 512, PAIR])
+        nc.gpsimd.tensor_scalar(rounded[1][:, :, last - 1 :], both, one[:], -0.0, ALU.mult, ALU.add)
 
         for c, copy in enumerate((nc.vector.tensor_copy, nc.scalar.copy)):
             lo, hi = OUT_CHUNKS[c]

from contextlib import ExitStack

import concourse.mybir as mybir

K, T, N, U = 512, 512, 512, 1024
FLOPS = 2 * 2 * K * N * T

F32 = mybir.dt.float32
BF16 = mybir.dt.bfloat16
I32 = mybir.dt.int32
U32 = mybir.dt.uint32
U16 = mybir.dt.uint16
U8 = mybir.dt.uint8
FP8X4 = mybir.dt.float8_e4m3fn_x4
ALU = mybir.AluOpType
ACT = mybir.ActivationFunctionType

P = 128
PACK = 4
QUADRANTS = 4
QUADRANT = 32
SCALE_ROWS = 4
PAIR = 2
OUT_CHUNKS = ((0, 512), (512, 1024))


def tile_picked_wgmem_tanh_lo_kernel(
    tc, x_words, x_scales, mem, w1, w2, slot, out_0, out_1, out_2
):
    nc = tc.nc
    mem_rows = mem.rearrange("(p t) u -> p t u", t=PACK)
    out_rows = out_0.rearrange("(p t) u -> p t u", t=PACK)
    out_words = out_1[0].rearrange("p u r -> p (u r)").bitcast(I32)

    with ExitStack() as ctx:
        keep = ctx.enter_context(tc.tile_pool(name="keep", bufs=1))
        psum = ctx.enter_context(tc.psum_pool(name="psum", bufs=1))

        offsets = keep.tile([P, T // 16], U16, name="offsets")
        window = [keep.tile([P, U], F32, name="window%d" % t) for t in range(PACK)]
        raw = {
            (which, piece): keep.tile([P, PAIR, N], F32, name="raw_%s%d" % (which, piece))
            for which in ("gate", "cand")
            for piece in range(2)
        }
        x_codes = keep.tile([P, T], U32, name="x_codes", align_bytes=64)
        x_plane = keep.tile([P, T], U8, name="x_plane", align_bytes=64)

        def load_weight(which, w, piece):
            nc.sync.dma_start(
                raw[which, piece][:], w.rearrange("(p j) m -> p j m", j=PACK)[:, PAIR * piece : PAIR * (piece + 1), :]
            )

        def load_window(t):
            nc.sync.dma_start(window[t][:], mem_rows[:, t, :])

        nc.vector.memset(x_plane[:].bitcast(U32), 0)
        nc.sync.dma_start(offsets[:], slot)
        load_weight("gate", w2, 0)
        for q in range(QUADRANTS):
            nc.sync.dma_start(
                x_plane[QUADRANT * q : QUADRANT * q + SCALE_ROWS, :].bitcast(I32),
                x_scales[0, SCALE_ROWS * q : SCALE_ROWS * (q + 1), :].bitcast(I32),
            )
        load_weight("gate", w2, 1)
        nc.sync.dma_start(x_codes[:].bitcast(I32), x_words[0].rearrange("p n r -> p (n r)").bitcast(I32))
        for t in range(PACK - 1):
            load_window(t)
        for piece in range(2):
            load_weight("cand", w1, piece)
        load_window(PACK - 1)

        span = {"gate": PACK, "cand": PAIR}
        dealt, codes, plane, acc = {}, {}, {}, {}
        for which in ("gate", "cand"):
            for g in range(PACK // span[which]):
                label = "%s%d" % (which, g)
                dealt[which, g] = keep.tile([P, span[which], P, PACK], BF16, name="dealt_" + label, tag="dealt_" + label, align_bytes=64)
                codes[which, g] = keep.tile([P, span[which] * P], U32, name="codes_" + label, align_bytes=64)
                if label != "cand1":
                    plane[which, g] = keep.tile([P, span[which] * P], U8, name="plane_" + label, align_bytes=64)

        def deal(which, g, piece, lo, hi, copy):
            copy(
                dealt[which, g][:].rearrange("p t m j -> p m j t")[:, lo:hi, PAIR * piece : PAIR * (piece + 1), :],
                raw[which, piece][:].rearrange("p j (m t) -> p m j t", t=PACK)[:, lo:hi, :, span[which] * g : span[which] * (g + 1)],
            )

        def quantize_weight(which, g):
            nc.vector.quantize_mx(
                out=codes[which, g][:].bitcast(FP8X4),
                scales=plane[which, g][:],
                in_=dealt[which, g][:].rearrange("p t m j -> p (t m j)"),
            )

        def multiply(which, t):
            g, cols = t // span[which], slice(P * (t % span[which]), P * (t % span[which] + 1))
            acc[which, t] = psum.tile([P, T], F32, name="acc_%s%d" % (which, t))
            nc.tensor.matmul_mx(
                out=acc[which, t][:],
                lhsT=codes[which, g][:, cols].bitcast(FP8X4),
                lhsT_scale=plane[which, g][:, cols],
                rhs=x_codes[:].bitcast(FP8X4),
                rhs_scale=x_plane[:],
                start=True,
                stop=True,
            )

        left = keep.tile([P, PAIR, T], F32, name="left")
        stay = [keep.tile([P, T], F32, name="stay%d" % t, tag="stay%d" % t, align_bytes=64) for t in range(PACK - 1)]
        cand = [keep.tile([P, T], F32, name="cand%d" % t) for t in range(PACK - 1)] + [left[:, 1, :]]
        new = [keep.tile([P, T], F32, name="new%d" % t) for t in range(PACK)]
        old = [keep.tile([P, T], F32, name="old%d" % t) for t in range(PACK - 1)] + [left[:, 0, :]]
        kept = {t: keep.tile([P, T], F32, name="kept%d" % t, tag="kept%d" % t) for t in (0, 1)}
        gate = {}
        moved = keep.tile([P, T], F32, name="moved")
        rounded = [
            keep.tile([P, hi - lo, PACK], BF16, name="rounded%d" % c, align_bytes=64) for c, (lo, hi) in enumerate(OUT_CHUNKS)
        ]
        words = [keep.tile([P, hi - lo], U32, name="words%d" % c, align_bytes=64) for c, (lo, hi) in enumerate(OUT_CHUNKS)]
        out_plane = keep.tile([P, U], U8, name="out_plane", align_bytes=64)

        def gather(t):
            nc.vector.tensor_copy(old[t][:], window[t][:].indirect(offsets[:]))

        def write_back(t):
            nc.vector.tensor_copy(window[t][:].indirect(offsets[:]), new[t][:])
            nc.sync.dma_start(out_rows[:, t, :], window[t][:])

        def round_out(t, c, copy):
            lo, hi = OUT_CHUNKS[c]
            if (t, c) == (PACK - 2, 0):
                both = window[t][:, lo:hi].rearrange("p (u o) -> p u o", o=1).to_broadcast([P, hi - lo, PAIR])
                copy(rounded[c][:, :, t:], both)
            else:
                copy(rounded[c][:, :, t], window[t][:, lo:hi])

        last = PACK - 1
        for piece in range(2):
            deal("gate", 0, piece, 0, 96, nc.vector.tensor_copy)
            deal("gate", 0, piece, 96, P, nc.scalar.copy)
        quantize_weight("gate", 0)
        for t in range(PACK):
            multiply("gate", t)
            if t < last:
                nc.scalar.activation(stay[t][:], acc["gate", t][:], ACT.Sigmoid, scale=-1.0)
        gate[1] = keep.tile([P, T], F32, name="gate1")
        nc.scalar.activation(gate[1][:], acc["gate", 1][:], ACT.Sigmoid)
        for t in range(last):
            gather(t)
        for t in range(2):
            nc.gpsimd.tensor_tensor(kept[t][:], old[t][:], stay[t][:], ALU.mult)
        for piece, copy in enumerate((nc.scalar.copy, nc.vector.tensor_copy)):
            for g in range(2):
                deal("cand", g, piece, 0, P, copy)
        quantize_weight("cand", 0)
        kept[2] = keep.tile([P, T], F32, name="kept2", tag="dealt_cand0", align_bytes=64)
        nc.gpsimd.tensor_tensor(kept[2][:], old[2][:], stay[2][:], ALU.mult)
        gather(last)
        plane["cand", 1] = keep.tile([P, PAIR * P], U8, name="plane_cand1", tag="stay2", align_bytes=64)
        quantize_weight("cand", 1)

        def candidate(t):
            multiply("cand", t)
            nc.scalar.activation(cand[t][:], acc["cand", t][:], ACT.Tanh)

        for t in range(PAIR):
            candidate(t)
        nc.vector.scalar_tensor_tensor(moved[:], stay[0][:], 1.0, cand[0][:], ALU.subtract, ALU.mult)
        for t in range(PAIR, PACK):
            candidate(t)
        for t in range(PACK):
            if t == 0:
                nc.vector.tensor_tensor(new[t][:], kept[t][:], moved[:], ALU.subtract)
                gate[2] = keep.tile([P, T], F32, name="gate2", tag="kept0")
                nc.scalar.activation(gate[2][:], acc["gate", 2][:], ACT.Sigmoid)
                right = keep.tile([P, PAIR, T], F32, name="right", tag="stay0", align_bytes=64)
                nc.scalar.activation(right[:, 0, :], acc["gate", last][:], ACT.Sigmoid, scale=-1.0)
                nc.scalar.activation(right[:, 1, :], acc["gate", last][:], ACT.Sigmoid)
            elif t < last:
                nc.gpsimd.tensor_tensor(moved[:], gate[t][:], cand[t][:], ALU.mult)
                nc.gpsimd.tensor_tensor(new[t][:], kept[t][:], moved[:], ALU.add)
            else:
                shares = keep.tile([P, PAIR, T], F32, name="shares", tag="dealt_cand0", align_bytes=64)
                nc.gpsimd.tensor_tensor(shares[:], left[:], right[:], ALU.mult)
                nc.gpsimd.tensor_tensor(new[t][:], shares[:, 0, :], shares[:, 1, :], ALU.add)
            write_back(t)
            if t < last:
                for c in range(len(OUT_CHUNKS)):
                    if (t, c) != (last - 1, 1):
                        round_out(t, c, nc.scalar.copy)
        one = keep.tile([P, 1], F32, name="one", tag="dealt_cand0", align_bytes=64)
        nc.gpsimd.memset(one[:], 1.0)
        both = window[last - 1][:, 512:].rearrange("p (u o) -> p u o", o=1).to_broadcast([P, 512, PAIR])
        nc.gpsimd.tensor_scalar(rounded[1][:, :, last - 1 :], both, one[:], -0.0, ALU.mult, ALU.add)

        for c, copy in enumerate((nc.vector.tensor_copy, nc.scalar.copy)):
            lo, hi = OUT_CHUNKS[c]
            for first in range(0, hi - lo, 256):
                copy(rounded[c][:, first : first + 256, last], window[last][:, lo + first : lo + first + 256])
        for c, (lo, hi) in enumerate(OUT_CHUNKS):
            for first in range(0, hi - lo, 256):
                nc.vector.quantize_mx(
                    out=words[c][:, first : first + 256].bitcast(FP8X4),
                    scales=out_plane[:, lo + first : lo + first + 256],
                    in_=rounded[c][:, first : first + 256, :].rearrange("p u t -> p (u t)"),
                )
                if c == 1:
                    nc.sync.dma_start(out_words[:, lo + first : lo + first + 256], words[c][:, first : first + 256].bitcast(I32))
            if c == 0:
                nc.sync.dma_start(out_words[:, lo:hi], words[c][:].bitcast(I32))
        for q in range(QUADRANTS):
            queue = nc.sync if q % 2 == 0 else nc.scalar
            queue.dma_start(
                out_2[0, SCALE_ROWS * q : SCALE_ROWS * (q + 1), :].bitcast(I32),
                out_plane[QUADRANT * q : QUADRANT * q + SCALE_ROWS, :].bitcast(I32),
            )
